import numpy as np
import ml_dtypes


def mxq(x, axis, fmt="e4m3"):
    dtype, down = {"e4m3": (ml_dtypes.float8_e4m3fn, 7), "e5m2": (ml_dtypes.float8_e5m2, 14)}[fmt]
    v = np.moveaxis(np.asarray(x, np.float32).astype(ml_dtypes.bfloat16).astype(np.float64), axis, -1)
    blocks = v.reshape(v.shape[:-1] + (-1, 32))
    amax = np.abs(blocks).max(-1, keepdims=True)
    byte = np.maximum(np.where(amax > 0, np.frexp(amax)[1] - 1 + 127, 0) - down, 1)
    scale = np.exp2(byte - 127.0)
    codes = (blocks / scale).astype(np.float32).astype(dtype).astype(np.float64)
    return np.moveaxis((codes * scale).reshape(v.shape), -1, axis)


WIDE = False


def mx_kscale(k):
    if not WIDE:
        return np.ones(k)
    levels = np.array([10, -10, 5, -5, 0])
    if k % 512:
        return np.exp2(np.random.permutation(np.resize(levels, k // 32))).repeat(32)
    a = np.empty((k // 512, 16))
    for p in range(k // 512):
        a[p, :8] = np.random.permutation(np.resize(levels, 8))
        for g in range(8):
            far = levels[np.abs(levels - a[p, g]) >= 10]
            a[p, g + 8] = far[np.random.randint(len(far))]
    return np.exp2(a.ravel()).repeat(32)


def f64(x):
    return np.asarray(x).astype(np.float64)


def striped(idx):
    return np.tile(np.asarray(idx).reshape(-1, 16).T, (8, 1)).astype(np.uint16)


def unstriped(offs):
    return offs[:16].T.reshape(-1).astype(np.int64)


B, N, T, D, NQ = 1, 512, 2048, 512, 256
DV = 512


def setup_inputs():
    n = np.random.standard_normal
    idx = np.sort(np.random.permutation(T)[:B * N].reshape(B, N), axis=1).reshape(-1)
    u = mx_kscale(N)
    ut = np.ones(T)
    ut[idx] = u
    return {
        "vT": (n((DV, T)) / ut).astype(np.float32),
        "wT": (np.random.dirichlet(np.ones(N), NQ).T[None] * u[:, None] * 16).astype(np.float32),
        "offs": striped(idx),
    }


def reference(vT, wT, offs):
    idx = unstriped(offs)
    pick = lambda x, which: x[:, which].reshape(x.shape[0], B, -1).transpose(1, 0, 2)
    wq = mxq(f64(wT), 1, "e4m3")
    o = wq.transpose(0, 2, 1) @ mxq(pick(f64(vT), idx).transpose(0, 2, 1), 1, "e4m3")
    m = np.max(o, axis=-1, keepdims=True)
    x = np.exp(o - m)
    r_ = x / np.sum(x, axis=-1, keepdims=True)
    return r_

@@ -1,0 +1,107 @@
+from contextlib import ExitStack
+
+import concourse.mybir as mybir
+from concourse.masks import make_identity
+
+F32 = mybir.dt.float32
+BF16 = mybir.dt.bfloat16
+U32 = mybir.dt.uint32
+U16 = mybir.dt.uint16
+U8 = mybir.dt.uint8
+FP8X4 = mybir.dt.float8_e4m3fn_x4
+ACT = mybir.ActivationFunctionType
+ALU = mybir.AluOpType
+AXIS = mybir.AxisListType
+
+P = 128
+SLOTS, TOKENS, QUERIES, FEATURES = 512, 2048, 256, 512
+FLOPS = 2 * QUERIES * SLOTS * FEATURES
+
+
+def tile_attend_wsum_soft_f_srt_kernel(tc, vT, wT, offs, out):
+    nc = tc.nc
+    e_blocks = FEATURES // P
+    q_blocks = QUERIES // P
+    with ExitStack() as ctx:
+        keep = ctx.enter_context(tc.tile_pool(name="keep", bufs=1))
+        psum = ctx.enter_context(tc.psum_pool(name="psum", bufs=1))
+
+        offsets = keep.tile([P, SLOTS // 16], U16, name="offsets")
+        pools = [keep.tile([P, TOKENS], F32, name="pool%d" % b) for b in range(e_blocks)]
+        w_raw = [keep.tile([P, 4, P], F32, name="w_raw%d" % h) for h in range(q_blocks)]
+        w_rows = wT[0].rearrange("(p j) q -> p j q", j=4)
+        nc.sync.dma_start(pools[0][:], vT[0:P, :])
+        nc.sync.dma_start(offsets[:], offs)
+        for b in range(1, e_blocks):
+            nc.sync.dma_start(pools[b][:], vT[b * P:(b + 1) * P, :])
+        for h in range(q_blocks):
+            nc.sync.dma_start(w_raw[h][:], w_rows[:, :, h * P:(h + 1) * P])
+
+        ident = keep.tile([P, P], F32, name="ident")
+        make_identity(nc, ident[:])
+
+        v_codes = keep.tile([P, FEATURES], U32, name="v_codes", align_bytes=64)
+        v_scales = keep.tile([P, FEATURES], U8, name="v_scales", align_bytes=64)
+        w_codes = keep.tile([P, QUERIES], U32, name="w_codes", align_bytes=64)
+        w_scales = keep.tile([P, QUERIES], U8, name="w_scales", align_bytes=64)
+        w_bf = [keep.tile([P, P, 4], BF16, name="w_bf%d" % h, align_bytes=64) for h in range(q_blocks)]
+        v_bf = [keep.tile([P, 4 * P], BF16, name="v_bf%d" % b, align_bytes=64) for b in range(e_blocks)]
+        picked = [keep.tile([P, 2, P, 2], BF16, name="picked%d" % b, align_bytes=64) for b in range(e_blocks)]
+        turned = [psum.tile([P, 2, P], F32, name="turned%d" % b) for b in range(e_blocks)]
+
+        def gather(b):
+            nc.vector.tensor_copy(picked[b][:].rearrange("e u p i -> e p u i"), pools[b][:].indirect(offsets[:]))
+
+        def turn(b):
+            words = picked[b][:].rearrange("e u p i -> e (u p i)").bitcast(F32)
+            for u in range(2):
+                nc.tensor.transpose(turned[b][:, u, :], words[:, u * P:(u + 1) * P], ident[:])
+
+        def copy_out(b, on_scalar):
+            dst = v_bf[b][:].bitcast(F32).rearrange("p (e u) -> p e u", u=2)
+            src = turned[b][:].rearrange("p u e -> p e u")
+            if on_scalar:
+                nc.scalar.copy(dst, src)
+            else:
+                nc.vector.tensor_copy(dst, src)
+
+        def quant_v(b):
+            cols = slice(b * P, (b + 1) * P)
+            nc.vector.quantize_mx(out=v_codes[:, cols].bitcast(FP8X4), scales=v_scales[:, cols], in_=v_bf[b][:])
+
+        def quant_w(h):
+            cols = slice(h * P, (h + 1) * P)
+            nc.vector.quantize_mx(out=w_codes[:, cols].bitcast(FP8X4), scales=w_scales[:, cols],
+                                  in_=w_bf[h][:].rearrange("p q j -> p (q j)"))
+
+        for b in range(e_blocks - 1):
+            gather(b)
+            turn(b)
+            copy_out(b, False)
+            quant_v(b)
+        last = e_blocks - 1
+        gather(last)
+        turn(last)
+        nc.scalar.activation(w_bf[0][:], w_raw[0][:].rearrange("p j q -> p q j"), ACT.Copy)
+        copy_out(last, True)
+        nc.vector.tensor_copy(w_bf[1][:], w_raw[1][:].rearrange("p j q -> p q j"))
+        quant_w(0)
+        quant_v(last)
+        quant_w(1)
+
+        for h in range(q_blocks):
+            rows = slice(h * P, (h + 1) * P)
+            logits = psum.tile([P, FEATURES], F32, name="logits%d" % h)
+            for c0, c1 in ((0, 256), (256, 384), (384, 512)):
+                nc.tensor.matmul_mx(out=logits[:, c0:c1], lhsT=w_codes[:, rows].bitcast(FP8X4), lhsT_scale=w_scales[:, rows],
+                                    rhs=v_codes[:, c0:c1].bitcast(FP8X4), rhs_scale=v_scales[:, c0:c1], start=True, stop=True)
+            neg_max = keep.tile([P, 1], F32, name="neg_max%d" % h)
+            nc.vector.tensor_reduce(neg_max[:], logits[:], AXIS.X, ALU.max, negate=True)
+            expd = keep.tile([P, FEATURES], F32, name="expd%d" % h)
+            total = keep.tile([P, 1], F32, name="total%d" % h)
+            nc.scalar.activation(expd[:], logits[:], ACT.Exp, bias=neg_max[:], scale=1.0, accum_out=total[:])
+            inv = keep.tile([P, 1], F32, name="inv%d" % h)
+            nc.vector.reciprocal(inv[:], total[:])
+            probs = keep.tile([P, FEATURES], F32, name="probs%d" % h)
+            nc.vector.tensor_scalar(probs[:], expd[:], inv[:], None, ALU.mult)
+            nc.sync.dma_start(out[0, rows, :], probs[:])

@@ -16,6 +16,8 @@ AXIS = mybir.AxisListType
 P = 128
 SLOTS, TOKENS, QUERIES, FEATURES = 512, 2048, 256, 512
 FLOPS = 2 * QUERIES * SLOTS * FEATURES
+V_PLACE = (0, 1, 2, 4)
+W_PLACE = (3, 5)
 
 
 def tile_attend_wsum_soft_f_srt_kernel(tc, vT, wT, offs, out):
@@ -32,76 +34,103 @@ def tile_attend_wsum_soft_f_srt_kernel(tc, vT, wT, offs, out):
         w_rows = wT[0].rearrange("(p j) q -> p j q", j=4)
         nc.sync.dma_start(pools[0][:], vT[0:P, :])
         nc.sync.dma_start(offsets[:], offs)
-        for b in range(1, e_blocks):
+        last = e_blocks - 1
+        reach = TOKENS - SLOTS // 2
+        for b in range(1, last):
             nc.sync.dma_start(pools[b][:], vT[b * P:(b + 1) * P, :])
+        nc.sync.dma_start(pools[last][:, :reach], vT[last * P:, :reach])
+        nc.sync.dma_start(pools[last][:, reach:], vT[last * P:, reach:])
         for h in range(q_blocks):
             nc.sync.dma_start(w_raw[h][:], w_rows[:, :, h * P:(h + 1) * P])
 
         ident = keep.tile([P, P], F32, name="ident")
         make_identity(nc, ident[:])
 
-        v_codes = keep.tile([P, FEATURES], U32, name="v_codes", align_bytes=64)
-        v_scales = keep.tile([P, FEATURES], U8, name="v_scales", align_bytes=64)
-        w_codes = keep.tile([P, QUERIES], U32, name="w_codes", align_bytes=64)
-        w_scales = keep.tile([P, QUERIES], U8, name="w_scales", align_bytes=64)
-        w_bf = [keep.tile([P, P, 4], BF16, name="w_bf%d" % h, align_bytes=64) for h in range(q_blocks)]
-        v_bf = [keep.tile([P, 4 * P], BF16, name="v_bf%d" % b, align_bytes=64) for b in range(e_blocks)]
+        places = e_blocks + q_blocks
+        codes = keep.tile([P, places * P], U32, name="codes", align_bytes=64)
+        scales = keep.tile([P, places * P], U8, name="scales", align_bytes=64)
+        rounded = keep.tile([P, places, 4 * P], BF16, name="rounded", align_bytes=64)
         picked = [keep.tile([P, 2, P, 2], BF16, name="picked%d" % b, align_bytes=64) for b in range(e_blocks)]
         turned = [psum.tile([P, 2, P], F32, name="turned%d" % b) for b in range(e_blocks)]
 
         def gather(b):
-            nc.vector.tensor_copy(picked[b][:].rearrange("e u p i -> e p u i"), pools[b][:].indirect(offsets[:]))
+            dst = picked[b][:].rearrange("e u p i -> e p u i")
+            if b < last:
+                nc.vector.tensor_copy(dst, pools[b][:].indirect(offsets[:]))
+            else:
+                nc.vector.tensor_copy(dst[:, :P // 2], pools[b][:, :reach].indirect(offsets[:, :SLOTS // 32]))
+                nc.vector.tensor_copy(dst[:, P // 2:], pools[b][:].indirect(offsets[:, SLOTS // 32:]))
 
         def turn(b):
             words = picked[b][:].rearrange("e u p i -> e (u p i)").bitcast(F32)
             for u in range(2):
                 nc.tensor.transpose(turned[b][:, u, :], words[:, u * P:(u + 1) * P], ident[:])
 
-        def copy_out(b, on_scalar):
-            dst = v_bf[b][:].bitcast(F32).rearrange("p (e u) -> p e u", u=2)
-            src = turned[b][:].rearrange("p u e -> p e u")
-            if on_scalar:
-                nc.scalar.copy(dst, src)
+        def copy_out(b):
+            dst = rounded[:, V_PLACE[b], :]
+            if b > 0:
+                nc.scalar.copy(dst.bitcast(F32).rearrange("p (e u) -> p e u", u=2), turned[b][:].rearrange("p u e -> p e u"))
             else:
-                nc.vector.tensor_copy(dst, src)
+                nc.scalar.activation(dst.rearrange("p (e u i) -> p e u i", u=2, i=2),
+                                     turned[b][:].rearrange("p u e -> p (u e)").bitcast(BF16).rearrange("p (u e i) -> p e u i", u=2, i=2),
+                                     ACT.Copy)
 
-        def quant_v(b):
-            cols = slice(b * P, (b + 1) * P)
-            nc.vector.quantize_mx(out=v_codes[:, cols].bitcast(FP8X4), scales=v_scales[:, cols], in_=v_bf[b][:])
+        def quantise(first, count):
+            cols = slice(first * P, (first + count) * P)
+            nc.vector.quantize_mx(out=codes[:, cols].bitcast(FP8X4), scales=scales[:, cols],
+                                  in_=rounded[:, first:first + count, :].rearrange("p c x -> p (c x)"))
 
-        def quant_w(h):
-            cols = slice(h * P, (h + 1) * P)
-            nc.vector.quantize_mx(out=w_codes[:, cols].bitcast(FP8X4), scales=w_scales[:, cols],
-                                  in_=w_bf[h][:].rearrange("p q j -> p (q j)"))
+        def w_views(h):
+            return rounded[:, W_PLACE[h], :].rearrange("p (q j) -> p q j", j=4), w_raw[h][:].rearrange("p j q -> p q j")
 
-        for b in range(e_blocks - 1):
+        for b in range(e_blocks):
             gather(b)
             turn(b)
-            copy_out(b, False)
-            quant_v(b)
-        last = e_blocks - 1
-        gather(last)
-        turn(last)
-        nc.scalar.activation(w_bf[0][:], w_raw[0][:].rearrange("p j q -> p q j"), ACT.Copy)
-        copy_out(last, True)
-        nc.vector.tensor_copy(w_bf[1][:], w_raw[1][:].rearrange("p j q -> p q j"))
-        quant_w(0)
-        quant_v(last)
-        quant_w(1)
+            if b < last:
+                copy_out(b)
+            if b == 2:
+                quantise(0, 2)
+        nc.scalar.activation(*w_views(0), ACT.Copy)
+        nc.vector.tensor_copy(*w_views(1))
+        copy_out(last)
+        quantise(2, 2)
+        quantise(W_PLACE[1], 1)
+        quantise(V_PLACE[last], 1)
 
-        for h in range(q_blocks):
-            rows = slice(h * P, (h + 1) * P)
-            logits = psum.tile([P, FEATURES], F32, name="logits%d" % h)
-            for c0, c1 in ((0, 256), (256, 384), (384, 512)):
-                nc.tensor.matmul_mx(out=logits[:, c0:c1], lhsT=w_codes[:, rows].bitcast(FP8X4), lhsT_scale=w_scales[:, rows],
-                                    rhs=v_codes[:, c0:c1].bitcast(FP8X4), rhs_scale=v_scales[:, c0:c1], start=True, stop=True)
-            neg_max = keep.tile([P, 1], F32, name="neg_max%d" % h)
-            nc.vector.tensor_reduce(neg_max[:], logits[:], AXIS.X, ALU.max, negate=True)
-            expd = keep.tile([P, FEATURES], F32, name="expd%d" % h)
-            total = keep.tile([P, 1], F32, name="total%d" % h)
-            nc.scalar.activation(expd[:], logits[:], ACT.Exp, bias=neg_max[:], scale=1.0, accum_out=total[:])
+        def product(dst, h, first, count):
+            rows = slice(W_PLACE[h] * P, (W_PLACE[h] + 1) * P)
+            cols = slice(V_PLACE[first] * P, (V_PLACE[first] + count) * P)
+            nc.tensor.matmul_mx(out=dst, lhsT=codes[:, rows].bitcast(FP8X4), lhsT_scale=scales[:, rows],
+                                rhs=codes[:, cols].bitcast(FP8X4), rhs_scale=scales[:, cols], start=True, stop=True)
+
+        early = last * P
+        logits0a = psum.tile([P, early], F32, name="logits0a")
+        logits0b = psum.tile([P, P], F32, name="logits0b")
+        logits1 = psum.tile([P, FEATURES], F32, name="logits1")
+        product(logits0a[:, 0:256], 0, 0, 2)
+        product(logits0a[:, 256:early], 0, 2, 1)
+        product(logits1[:, 0:256], 1, 0, 2)
+        product(logits1[:, 256:early], 1, 2, 1)
+        product(logits0b[:], 0, last, 1)
+        product(logits1[:, early:], 1, last, 1)
+
+        neg_max = [keep.tile([P, 1], F32, name="neg_max%d" % h) for h in range(q_blocks)]
+        neg_max_early = keep.tile([P, 1], F32, name="neg_max_early")
+        neg_logits0 = keep.tile([P, FEATURES], F32, name="neg_logits0")
+        nc.vector.tensor_scalar(neg_logits0[:, :early], logits0a[:], -1.0, None, ALU.mult, ALU.min, accum_out=neg_max_early[:])
+        nc.vector.tensor_scalar(neg_logits0[:, early:], logits0b[:], -1.0, neg_max_early[:], ALU.mult, ALU.min, accum_out=neg_max[0][:])
+        nc.vector.tensor_reduce(neg_max[1][:], logits1[:], AXIS.X, ALU.max, negate=True)
+
+        expd = [keep.tile([P, FEATURES], F32, name="expd%d" % h) for h in range(q_blocks)]
+        total = [keep.tile([P, 1], F32, name="total%d" % h) for h in range(q_blocks)]
+        nc.scalar.activation(expd[0][:], neg_logits0[:], ACT.Exp, bias=neg_max[0][:], scale=-1.0, accum_out=total[0][:])
+        nc.scalar.activation(expd[1][:], logits1[:], ACT.Exp, bias=neg_max[1][:], scale=1.0, accum_out=total[1][:])
+        for h, pieces in ((0, 1), (1, 2)):
             inv = keep.tile([P, 1], F32, name="inv%d" % h)
-            nc.vector.reciprocal(inv[:], total[:])
+            nc.vector.reciprocal(inv[:], total[h][:])
             probs = keep.tile([P, FEATURES], F32, name="probs%d" % h)
-            nc.vector.tensor_scalar(probs[:], expd[:], inv[:], None, ALU.mult)
-            nc.sync.dma_start(out[0, rows, :], probs[:])
+            width = FEATURES // pieces
+            for c in range(pieces):
+                cols = slice(c * width, (c + 1) * width)
+                nc.vector.tensor_scalar(probs[:, cols], expd[h][:, cols], inv[:], None, ALU.mult)
+                nc.sync.dma_start(out[0, h * P:(h + 1) * P, cols], probs[:, cols])

@@ -16,42 +16,39 @@ AXIS = mybir.AxisListType
 P = 128
 SLOTS, TOKENS, QUERIES, FEATURES = 512, 2048, 256, 512
 FLOPS = 2 * QUERIES * SLOTS * FEATURES
-V_PLACE = (0, 1, 2, 4)
-W_PLACE = (3, 5)
 
 
 def tile_attend_wsum_soft_f_srt_kernel(tc, vT, wT, offs, out):
     nc = tc.nc
     e_blocks = FEATURES // P
     q_blocks = QUERIES // P
+    last = e_blocks - 1
+    reach = TOKENS - SLOTS // 2
     with ExitStack() as ctx:
         keep = ctx.enter_context(tc.tile_pool(name="keep", bufs=1))
         psum = ctx.enter_context(tc.psum_pool(name="psum", bufs=1))
 
         offsets = keep.tile([P, SLOTS // 16], U16, name="offsets")
-        pools = [keep.tile([P, TOKENS], F32, name="pool%d" % b) for b in range(e_blocks)]
-        w_raw = [keep.tile([P, 4, P], F32, name="w_raw%d" % h) for h in range(q_blocks)]
-        w_rows = wT[0].rearrange("(p j) q -> p j q", j=4)
+        pools = [keep.tile([P, TOKENS], F32, name="pool%d" % b, tag="pool%d" % b, align_bytes=64) for b in range(e_blocks)]
+        w_raw = keep.tile([P, 4, QUERIES], F32, name="w_raw", tag="w_raw", align_bytes=64)
         nc.sync.dma_start(pools[0][:], vT[0:P, :])
         nc.sync.dma_start(offsets[:], offs)
-        last = e_blocks - 1
-        reach = TOKENS - SLOTS // 2
         for b in range(1, last):
             nc.sync.dma_start(pools[b][:], vT[b * P:(b + 1) * P, :])
         nc.sync.dma_start(pools[last][:, :reach], vT[last * P:, :reach])
         nc.sync.dma_start(pools[last][:, reach:], vT[last * P:, reach:])
-        for h in range(q_blocks):
-            nc.sync.dma_start(w_raw[h][:], w_rows[:, :, h * P:(h + 1) * P])
+        nc.sync.dma_start(w_raw[:], wT[0].rearrange("(p j) q -> p j q", j=4))
 
         ident = keep.tile([P, P], F32, name="ident")
         make_identity(nc, ident[:])
 
-        places = e_blocks + q_blocks
-        codes = keep.tile([P, places * P], U32, name="codes", align_bytes=64)
-        scales = keep.tile([P, places * P], U8, name="scales", align_bytes=64)
-        rounded = keep.tile([P, places, 4 * P], BF16, name="rounded", align_bytes=64)
         picked = [keep.tile([P, 2, P, 2], BF16, name="picked%d" % b, align_bytes=64) for b in range(e_blocks)]
         turned = [psum.tile([P, 2, P], F32, name="turned%d" % b) for b in range(e_blocks)]
+        v_scales = keep.tile([P, FEATURES], U8, name="v_scales", align_bytes=64)
+        w_scales = keep.tile([P, QUERIES], U8, name="w_scales", align_bytes=64)
+        w_codes = keep.tile([P, QUERIES], U32, name="w_codes", align_bytes=64)
+        w_bf = keep.tile([P, QUERIES, 4], BF16, name="w_bf", align_bytes=64)
+        v_bf, v_codes = {}, {}
 
         def gather(b):
             dst = picked[b][:].rearrange("e u p i -> e p u i")
@@ -67,70 +64,61 @@ def tile_attend_wsum_soft_f_srt_kernel(tc, vT, wT, offs, out):
                 nc.tensor.transpose(turned[b][:, u, :], words[:, u * P:(u + 1) * P], ident[:])
 
         def copy_out(b):
-            dst = rounded[:, V_PLACE[b], :]
+            v_bf[b] = keep.tile([P, 4 * P], BF16, name="v_bf%d" % b, tag="w_raw" if b == last else "v_bf%d" % b, align_bytes=64)
             if b > 0:
-                nc.scalar.copy(dst.bitcast(F32).rearrange("p (e u) -> p e u", u=2), turned[b][:].rearrange("p u e -> p e u"))
+                nc.scalar.copy(v_bf[b][:].bitcast(F32).rearrange("p (e u) -> p e u", u=2), turned[b][:].rearrange("p u e -> p e u"))
             else:
-                nc.scalar.activation(dst.rearrange("p (e u i) -> p e u i", u=2, i=2),
+                nc.scalar.activation(v_bf[b][:].rearrange("p (e u i) -> p e u i", u=2, i=2),
                                      turned[b][:].rearrange("p u e -> p (u e)").bitcast(BF16).rearrange("p (u e i) -> p e u i", u=2, i=2),
                                      ACT.Copy)
 
-        def quantise(first, count):
-            cols = slice(first * P, (first + count) * P)
-            nc.vector.quantize_mx(out=codes[:, cols].bitcast(FP8X4), scales=scales[:, cols],
-                                  in_=rounded[:, first:first + count, :].rearrange("p c x -> p (c x)"))
+        def quantise_v(b):
+            v_codes[b] = keep.tile([P, P], U32, name="v_codes%d" % b, tag="pool%d" % (b + 1), align_bytes=64)
+            nc.vector.quantize_mx(out=v_codes[b][:].bitcast(FP8X4), scales=v_scales[:, b * P:(b + 1) * P], in_=v_bf[b][:])
 
-        def w_views(h):
-            return rounded[:, W_PLACE[h], :].rearrange("p (q j) -> p q j", j=4), w_raw[h][:].rearrange("p j q -> p q j")
+        def quantise_w(h):
+            rows = slice(h * P, (h + 1) * P)
+            nc.vector.quantize_mx(out=w_codes[:, rows].bitcast(FP8X4), scales=w_scales[:, rows], in_=w_bf[:, rows, :].rearrange("p q j -> p (q j)"))
+
+        def w_views(q0, q1):
+            return w_bf[:, q0:q1, :], w_raw[:, :, q0:q1].rearrange("p j q -> p q j")
+
+        logits = [psum.tile([P, FEATURES], F32, name="logits%d" % h) for h in range(q_blocks)]
+
+        def product(h, b):
+            rows = slice(h * P, (h + 1) * P)
+            cols = slice(b * P, (b + 1) * P)
+            nc.tensor.matmul_mx(out=logits[h][:, cols], lhsT=w_codes[:, rows].bitcast(FP8X4), lhsT_scale=w_scales[:, rows],
+                                rhs=v_codes[b][:].bitcast(FP8X4), rhs_scale=v_scales[:, cols], start=True, stop=True)
 
         for b in range(e_blocks):
             gather(b)
             turn(b)
             if b < last:
                 copy_out(b)
-            if b == 2:
-                quantise(0, 2)
-        nc.scalar.activation(*w_views(0), ACT.Copy)
-        nc.vector.tensor_copy(*w_views(1))
+            if b > 0:
+                quantise_v(b - 1)
+        nc.vector.tensor_copy(*w_views(0, P))
+        nc.vector.tensor_copy(*w_views(P, P + P // 2))
+        nc.scalar.activation(*w_views(P + P // 2, QUERIES), ACT.Copy)
         copy_out(last)
-        quantise(2, 2)
-        quantise(W_PLACE[1], 1)
-        quantise(V_PLACE[last], 1)
+        quantise_w(0)
+        quantise_w(1)
+        quantise_v(last)
+        for h in range(q_blocks):
+            for b in range(last):
+                product(h, b)
+        for h in range(q_blocks):
+            product(h, last)
 
-        def product(dst, h, first, count):
-            rows = slice(W_PLACE[h] * P, (W_PLACE[h] + 1) * P)
-            cols = slice(V_PLACE[first] * P, (V_PLACE[first] + count) * P)
-            nc.tensor.matmul_mx(out=dst, lhsT=codes[:, rows].bitcast(FP8X4), lhsT_scale=scales[:, rows],
-                                rhs=codes[:, cols].bitcast(FP8X4), rhs_scale=scales[:, cols], start=True, stop=True)
-
-        early = last * P
-        logits0a = psum.tile([P, early], F32, name="logits0a")
-        logits0b = psum.tile([P, P], F32, name="logits0b")
-        logits1 = psum.tile([P, FEATURES], F32, name="logits1")
-        product(logits0a[:, 0:256], 0, 0, 2)
-        product(logits0a[:, 256:early], 0, 2, 1)
-        product(logits1[:, 0:256], 1, 0, 2)
-        product(logits1[:, 256:early], 1, 2, 1)
-        product(logits0b[:], 0, last, 1)
-        product(logits1[:, early:], 1, last, 1)
-
-        neg_max = [keep.tile([P, 1], F32, name="neg_max%d" % h) for h in range(q_blocks)]
-        neg_max_early = keep.tile([P, 1], F32, name="neg_max_early")
-        neg_logits0 = keep.tile([P, FEATURES], F32, name="neg_logits0")
-        nc.vector.tensor_scalar(neg_logits0[:, :early], logits0a[:], -1.0, None, ALU.mult, ALU.min, accum_out=neg_max_early[:])
-        nc.vector.tensor_scalar(neg_logits0[:, early:], logits0b[:], -1.0, neg_max_early[:], ALU.mult, ALU.min, accum_out=neg_max[0][:])
-        nc.vector.tensor_reduce(neg_max[1][:], logits1[:], AXIS.X, ALU.max, negate=True)
-
-        expd = [keep.tile([P, FEATURES], F32, name="expd%d" % h) for h in range(q_blocks)]
-        total = [keep.tile([P, 1], F32, name="total%d" % h) for h in range(q_blocks)]
-        nc.scalar.activation(expd[0][:], neg_logits0[:], ACT.Exp, bias=neg_max[0][:], scale=-1.0, accum_out=total[0][:])
-        nc.scalar.activation(expd[1][:], logits1[:], ACT.Exp, bias=neg_max[1][:], scale=1.0, accum_out=total[1][:])
-        for h, pieces in ((0, 1), (1, 2)):
+        for h in range(q_blocks):
+            neg_max = keep.tile([P, 1], F32, name="neg_max%d" % h)
+            nc.vector.tensor_reduce(neg_max[:], logits[h][:], AXIS.X, ALU.max, negate=True)
+            expd = keep.tile([P, FEATURES], F32, name="expd%d" % h)
+            total = keep.tile([P, 1], F32, name="total%d" % h)
+            nc.scalar.activation(expd[:], logits[h][:], ACT.Exp, bias=neg_max[:], scale=1.0, accum_out=total[:])
             inv = keep.tile([P, 1], F32, name="inv%d" % h)
-            nc.vector.reciprocal(inv[:], total[h][:])
+            nc.vector.reciprocal(inv[:], total[:])
             probs = keep.tile([P, FEATURES], F32, name="probs%d" % h)
-            width = FEATURES // pieces
-            for c in range(pieces):
-                cols = slice(c * width, (c + 1) * width)
-                nc.vector.tensor_scalar(probs[:, cols], expd[h][:, cols], inv[:], None, ALU.mult)
-                nc.sync.dma_start(out[0, h * P:(h + 1) * P, cols], probs[:, cols])
+            nc.vector.tensor_scalar(probs[:], expd[:], inv[:], None, ALU.mult)
+            nc.sync.dma_start(out[0, h * P:(h + 1) * P, :], probs[:])

@@ -23,7 +23,6 @@ def tile_attend_wsum_soft_f_srt_kernel(tc, vT, wT, offs, out):
     e_blocks = FEATURES // P
     q_blocks = QUERIES // P
     last = e_blocks - 1
-    reach = TOKENS - SLOTS // 2
     with ExitStack() as ctx:
         keep = ctx.enter_context(tc.tile_pool(name="keep", bufs=1))
         psum = ctx.enter_context(tc.psum_pool(name="psum", bufs=1))
@@ -35,14 +34,13 @@ def tile_attend_wsum_soft_f_srt_kernel(tc, vT, wT, offs, out):
         nc.sync.dma_start(offsets[:], offs)
         for b in range(1, last):
             nc.sync.dma_start(pools[b][:], vT[b * P:(b + 1) * P, :])
-        nc.sync.dma_start(pools[last][:, :reach], vT[last * P:, :reach])
-        nc.sync.dma_start(pools[last][:, reach:], vT[last * P:, reach:])
+        nc.sync.dma_start(pools[last][:], vT[last * P:, :])
         nc.sync.dma_start(w_raw[:], wT[0].rearrange("(p j) q -> p j q", j=4))
 
         ident = keep.tile([P, P], F32, name="ident")
         make_identity(nc, ident[:])
 
-        picked = [keep.tile([P, 2, P, 2], BF16, name="picked%d" % b, align_bytes=64) for b in range(e_blocks)]
+        picked = [keep.tile([P, SLOTS], BF16, name="picked%d" % b, align_bytes=64) for b in range(e_blocks)]
         turned = [psum.tile([P, 2, P], F32, name="turned%d" % b) for b in range(e_blocks)]
         v_scales = keep.tile([P, FEATURES], U8, name="v_scales", align_bytes=64)
         w_scales = keep.tile([P, QUERIES], U8, name="w_scales", align_bytes=64)
@@ -51,17 +49,12 @@ def tile_attend_wsum_soft_f_srt_kernel(tc, vT, wT, offs, out):
         v_bf, v_codes = {}, {}
 
         def gather(b):
-            dst = picked[b][:].rearrange("e u p i -> e p u i")
-            if b < last:
-                nc.vector.tensor_copy(dst, pools[b][:].indirect(offsets[:]))
-            else:
-                nc.vector.tensor_copy(dst[:, :P // 2], pools[b][:, :reach].indirect(offsets[:, :SLOTS // 32]))
-                nc.vector.tensor_copy(dst[:, P // 2:], pools[b][:].indirect(offsets[:, SLOTS // 32:]))
+            nc.vector.tensor_copy(picked[b][:], pools[b][:].indirect(offsets[:]))
 
         def turn(b):
-            words = picked[b][:].rearrange("e u p i -> e (u p i)").bitcast(F32)
+            words = picked[b][:].bitcast(F32)
             for u in range(2):
-                nc.tensor.transpose(turned[b][:, u, :], words[:, u * P:(u + 1) * P], ident[:])
+                nc.tensor.transpose(turned[b][:, u, :], words[:, u::2], ident[:])
 
         def copy_out(b):
             v_bf[b] = keep.tile([P, 4 * P], BF16, name="v_bf%d" % b, tag="w_raw" if b == last else "v_bf%d" % b, align_bytes=64)

@@ -23,13 +23,15 @@ def tile_attend_wsum_soft_f_srt_kernel(tc, vT, wT, offs, out):
     e_blocks = FEATURES // P
     q_blocks = QUERIES // P
     last = e_blocks - 1
+    early = last * P
     with ExitStack() as ctx:
         keep = ctx.enter_context(tc.tile_pool(name="keep", bufs=1))
+        shared = ctx.enter_context(tc.tile_pool(name="shared", bufs=1))
         psum = ctx.enter_context(tc.psum_pool(name="psum", bufs=1))
 
         offsets = keep.tile([P, SLOTS // 16], U16, name="offsets")
         pools = [keep.tile([P, TOKENS], F32, name="pool%d" % b, tag="pool%d" % b, align_bytes=64) for b in range(e_blocks)]
-        w_raw = keep.tile([P, 4, QUERIES], F32, name="w_raw", tag="w_raw", align_bytes=64)
+        w_raw = shared.tile([P, 4, QUERIES], F32, name="w_raw", offset=0, align_bytes=64)
         nc.sync.dma_start(pools[0][:], vT[0:P, :])
         nc.sync.dma_start(offsets[:], offs)
         for b in range(1, last):
@@ -45,7 +47,7 @@ def tile_attend_wsum_soft_f_srt_kernel(tc, vT, wT, offs, out):
         v_scales = keep.tile([P, FEATURES], U8, name="v_scales", align_bytes=64)
         w_scales = keep.tile([P, QUERIES], U8, name="w_scales", align_bytes=64)
         w_codes = keep.tile([P, QUERIES], U32, name="w_codes", align_bytes=64)
-        w_bf = keep.tile([P, QUERIES, 4], BF16, name="w_bf", align_bytes=64)
+        w_bf = [keep.tile([P, P, 4], BF16, name="w_bf%d" % h, align_bytes=64) for h in range(q_blocks)]
         v_bf, v_codes = {}, {}
 
         def gather(b):
@@ -57,7 +59,10 @@ def tile_attend_wsum_soft_f_srt_kernel(tc, vT, wT, offs, out):
                 nc.tensor.transpose(turned[b][:, u, :], words[:, u::2], ident[:])
 
         def copy_out(b):
-            v_bf[b] = keep.tile([P, 4 * P], BF16, name="v_bf%d" % b, tag="w_raw" if b == last else "v_bf%d" % b, align_bytes=64)
+            if b == last:
+                v_bf[b] = shared.tile([P, 4 * P], BF16, name="v_bf%d" % b, offset=0, align_bytes=64)
+            else:
+                v_bf[b] = keep.tile([P, 4 * P], BF16, name="v_bf%d" % b, align_bytes=64)
             if b > 0:
                 nc.scalar.copy(v_bf[b][:].bitcast(F32).rearrange("p (e u) -> p e u", u=2), turned[b][:].rearrange("p u e -> p e u"))
             else:
@@ -66,22 +71,26 @@ def tile_attend_wsum_soft_f_srt_kernel(tc, vT, wT, offs, out):
                                      ACT.Copy)
 
         def quantise_v(b):
-            v_codes[b] = keep.tile([P, P], U32, name="v_codes%d" % b, tag="pool%d" % (b + 1), align_bytes=64)
+            if b == last - 1:
+                v_codes[b] = shared.tile([P, P], U32, name="v_codes%d" % b, offset=2048, align_bytes=64)
+            else:
+                v_codes[b] = keep.tile([P, P], U32, name="v_codes%d" % b, tag="pool%d" % (b + 1), align_bytes=64)
             nc.vector.quantize_mx(out=v_codes[b][:].bitcast(FP8X4), scales=v_scales[:, b * P:(b + 1) * P], in_=v_bf[b][:])
 
         def quantise_w(h):
             rows = slice(h * P, (h + 1) * P)
-            nc.vector.quantize_mx(out=w_codes[:, rows].bitcast(FP8X4), scales=w_scales[:, rows], in_=w_bf[:, rows, :].rearrange("p q j -> p (q j)"))
+            nc.vector.quantize_mx(out=w_codes[:, rows].bitcast(FP8X4), scales=w_scales[:, rows], in_=w_bf[h][:].rearrange("p q j -> p (q j)"))
 
-        def w_views(q0, q1):
-            return w_bf[:, q0:q1, :], w_raw[:, :, q0:q1].rearrange("p j q -> p q j")
+        def w_views(h):
+            return w_bf[h][:], w_raw[:, :, h * P:(h + 1) * P].rearrange("p j q -> p q j")
 
         logits = [psum.tile([P, FEATURES], F32, name="logits%d" % h) for h in range(q_blocks)]
+        logits_last = psum.tile([P, P], F32, name="logits_last")
 
         def product(h, b):
             rows = slice(h * P, (h + 1) * P)
             cols = slice(b * P, (b + 1) * P)
-            nc.tensor.matmul_mx(out=logits[h][:, cols], lhsT=w_codes[:, rows].bitcast(FP8X4), lhsT_scale=w_scales[:, rows],
+            nc.tensor.matmul_mx(out=logits_last[:] if (h, b) == (0, last) else logits[h][:, cols], lhsT=w_codes[:, rows].bitcast(FP8X4), lhsT_scale=w_scales[:, rows],
                                 rhs=v_codes[b][:].bitcast(FP8X4), rhs_scale=v_scales[:, cols], start=True, stop=True)
 
         for b in range(e_blocks):
@@ -89,13 +98,13 @@ def tile_attend_wsum_soft_f_srt_kernel(tc, vT, wT, offs, out):
             turn(b)
             if b < last:
                 copy_out(b)
-            if b > 0:
+            if 0 < b < last:
                 quantise_v(b - 1)
-        nc.vector.tensor_copy(*w_views(0, P))
-        nc.vector.tensor_copy(*w_views(P, P + P // 2))
-        nc.scalar.activation(*w_views(P + P // 2, QUERIES), ACT.Copy)
+        nc.vector.tensor_copy(*w_views(0))
+        nc.scalar.activation(*w_views(1), ACT.Copy)
         copy_out(last)
         quantise_w(0)
+        quantise_v(last - 1)
         quantise_w(1)
         quantise_v(last)
         for h in range(q_blocks):
@@ -104,14 +113,22 @@ def tile_attend_wsum_soft_f_srt_kernel(tc, vT, wT, offs, out):
         for h in range(q_blocks):
             product(h, last)
 
-        for h in range(q_blocks):
-            neg_max = keep.tile([P, 1], F32, name="neg_max%d" % h)
-            nc.vector.tensor_reduce(neg_max[:], logits[h][:], AXIS.X, ALU.max, negate=True)
-            expd = keep.tile([P, FEATURES], F32, name="expd%d" % h)
-            total = keep.tile([P, 1], F32, name="total%d" % h)
-            nc.scalar.activation(expd[:], logits[h][:], ACT.Exp, bias=neg_max[:], scale=1.0, accum_out=total[:])
-            inv = keep.tile([P, 1], F32, name="inv%d" % h)
-            nc.vector.reciprocal(inv[:], total[:])
-            probs = keep.tile([P, FEATURES], F32, name="probs%d" % h)
-            nc.vector.tensor_scalar(probs[:], expd[:], inv[:], None, ALU.mult)
-            nc.sync.dma_start(out[0, h * P:(h + 1) * P, :], probs[:])
+        negated = keep.tile([P, FEATURES], F32, name="negated", align_bytes=64)
+        early_max = keep.tile([P, 1], F32, name="early_max")
+        neg_max = [keep.tile([P, 1], F32, name="neg_max%d" % h) for h in range(q_blocks)]
+        expd = [keep.tile([P, FEATURES], F32, name="expd%d" % h, align_bytes=64) for h in range(q_blocks)]
+        probs = [keep.tile([P, FEATURES], F32, name="probs%d" % h, align_bytes=64) for h in range(q_blocks)]
+        total = [keep.tile([P, 1], F32, name="total%d" % h) for h in range(q_blocks)]
+        inv = [keep.tile([P, 1], F32, name="inv%d" % h) for h in range(q_blocks)]
+        nc.vector.tensor_scalar(negated[:, :early], logits[0][:, :early], -1.0, None, ALU.mult, ALU.min, accum_out=early_max[:])
+        nc.vector.tensor_scalar(negated[:, early:], logits_last[:], -1.0, early_max[:], ALU.mult, ALU.min, accum_out=neg_max[0][:])
+        nc.vector.tensor_reduce(neg_max[1][:], logits[1][:], AXIS.X, ALU.max, negate=True)
+        nc.scalar.activation(expd[0][:], negated[:], ACT.Exp, bias=neg_max[0][:], scale=-1.0, accum_out=total[0][:])
+        nc.scalar.activation(expd[1][:], logits[1][:], ACT.Exp, bias=neg_max[1][:], scale=1.0, accum_out=total[1][:])
+        nc.vector.reciprocal(inv[0][:], total[0][:])
+        nc.vector.tensor_scalar(probs[0][:], expd[0][:], inv[0][:], None, ALU.mult)
+        nc.sync.dma_start(out[0, :P, :], probs[0][:])
+        nc.vector.reciprocal(inv[1][:], total[1][:])
+        nc.vector.tensor_scalar(probs[1][:, :early], expd[1][:, :early], inv[1][:], None, ALU.mult)
+        nc.scalar.activation(probs[1][:, early:], expd[1][:, early:], ACT.Copy, scale=inv[1][:])
+        nc.sync.dma_start(out[0, P:, :], probs[1][:])

@@ -129,6 +129,5 @@ def tile_attend_wsum_soft_f_srt_kernel(tc, vT, wT, offs, out):
         nc.vector.tensor_scalar(probs[0][:], expd[0][:], inv[0][:], None, ALU.mult)
         nc.sync.dma_start(out[0, :P, :], probs[0][:])
         nc.vector.reciprocal(inv[1][:], total[1][:])
-        nc.vector.tensor_scalar(probs[1][:, :early], expd[1][:, :early], inv[1][:], None, ALU.mult)
-        nc.scalar.activation(probs[1][:, early:], expd[1][:, early:], ACT.Copy, scale=inv[1][:])
+        nc.vector.tensor_scalar(probs[1][:], expd[1][:], inv[1][:], None, ALU.mult)
         nc.sync.dma_start(out[0, P:, :], probs[1][:])

@@ -23,15 +23,13 @@ def tile_attend_wsum_soft_f_srt_kernel(tc, vT, wT, offs, out):
     e_blocks = FEATURES // P
     q_blocks = QUERIES // P
     last = e_blocks - 1
-    early = last * P
     with ExitStack() as ctx:
         keep = ctx.enter_context(tc.tile_pool(name="keep", bufs=1))
-        shared = ctx.enter_context(tc.tile_pool(name="shared", bufs=1))
         psum = ctx.enter_context(tc.psum_pool(name="psum", bufs=1))
 
         offsets = keep.tile([P, SLOTS // 16], U16, name="offsets")
         pools = [keep.tile([P, TOKENS], F32, name="pool%d" % b, tag="pool%d" % b, align_bytes=64) for b in range(e_blocks)]
-        w_raw = shared.tile([P, 4, QUERIES], F32, name="w_raw", offset=0, align_bytes=64)
+        w_raw = keep.tile([P, 4, QUERIES], F32, name="w_raw", tag="w_raw", align_bytes=64)
         nc.sync.dma_start(pools[0][:], vT[0:P, :])
         nc.sync.dma_start(offsets[:], offs)
         for b in range(1, last):
@@ -47,7 +45,7 @@ def tile_attend_wsum_soft_f_srt_kernel(tc, vT, wT, offs, out):
         v_scales = keep.tile([P, FEATURES], U8, name="v_scales", align_bytes=64)
         w_scales = keep.tile([P, QUERIES], U8, name="w_scales", align_bytes=64)
         w_codes = keep.tile([P, QUERIES], U32, name="w_codes", align_bytes=64)
-        w_bf = [keep.tile([P, P, 4], BF16, name="w_bf%d" % h, align_bytes=64) for h in range(q_blocks)]
+        w_bf = [keep.tile([P, P, 4], BF16, name="w_bf%d" % h, tag="w_bf%d" % h, align_bytes=64) for h in range(q_blocks)]
         v_bf, v_codes = {}, {}
 
         def gather(b):
@@ -59,10 +57,7 @@ def tile_attend_wsum_soft_f_srt_kernel(tc, vT, wT, offs, out):
                 nc.tensor.transpose(turned[b][:, u, :], words[:, u::2], ident[:])
 
         def copy_out(b):
-            if b == last:
-                v_bf[b] = shared.tile([P, 4 * P], BF16, name="v_bf%d" % b, offset=0, align_bytes=64)
-            else:
-                v_bf[b] = keep.tile([P, 4 * P], BF16, name="v_bf%d" % b, align_bytes=64)
+            v_bf[b] = keep.tile([P, 4 * P], BF16, name="v_bf%d" % b, align_bytes=64)
             if b > 0:
                 nc.scalar.copy(v_bf[b][:].bitcast(F32).rearrange("p (e u) -> p e u", u=2), turned[b][:].rearrange("p u e -> p e u"))
             else:
@@ -71,10 +66,7 @@ def tile_attend_wsum_soft_f_srt_kernel(tc, vT, wT, offs, out):
                                      ACT.Copy)
 
         def quantise_v(b):
-            if b == last - 1:
-                v_codes[b] = shared.tile([P, P], U32, name="v_codes%d" % b, offset=2048, align_bytes=64)
-            else:
-                v_codes[b] = keep.tile([P, P], U32, name="v_codes%d" % b, tag="pool%d" % (b + 1), align_bytes=64)
+            v_codes[b] = keep.tile([P, P], U32, name="v_codes%d" % b, tag=["pool1", "pool2", "w_raw", "w_bf1"][b], align_bytes=64)
             nc.vector.quantize_mx(out=v_codes[b][:].bitcast(FP8X4), scales=v_scales[:, b * P:(b + 1) * P], in_=v_bf[b][:])
 
         def quantise_w(h):
@@ -82,15 +74,15 @@ def tile_attend_wsum_soft_f_srt_kernel(tc, vT, wT, offs, out):
             nc.vector.quantize_mx(out=w_codes[:, rows].bitcast(FP8X4), scales=w_scales[:, rows], in_=w_bf[h][:].rearrange("p q j -> p (q j)"))
 
         def w_views(h):
-            return w_bf[h][:], w_raw[:, :, h * P:(h + 1) * P].rearrange("p j q -> p q j")
+            return (w_bf[h][:].rearrange("p (c i) j -> p c j i", i=4),
+                    w_raw[:, :, h * P:(h + 1) * P].rearrange("p j (c i) -> p c j i", i=4))
 
         logits = [psum.tile([P, FEATURES], F32, name="logits%d" % h) for h in range(q_blocks)]
-        logits_last = psum.tile([P, P], F32, name="logits_last")
 
         def product(h, b):
             rows = slice(h * P, (h + 1) * P)
             cols = slice(b * P, (b + 1) * P)
-            nc.tensor.matmul_mx(out=logits_last[:] if (h, b) == (0, last) else logits[h][:, cols], lhsT=w_codes[:, rows].bitcast(FP8X4), lhsT_scale=w_scales[:, rows],
+            nc.tensor.matmul_mx(out=logits[h][:, cols], lhsT=w_codes[:, rows].bitcast(FP8X4), lhsT_scale=w_scales[:, rows],
                                 rhs=v_codes[b][:].bitcast(FP8X4), rhs_scale=v_scales[:, cols], start=True, stop=True)
 
         for b in range(e_blocks):
@@ -101,7 +93,7 @@ def tile_attend_wsum_soft_f_srt_kernel(tc, vT, wT, offs, out):
             if 0 < b < last:
                 quantise_v(b - 1)
         nc.vector.tensor_copy(*w_views(0))
-        nc.scalar.activation(*w_views(1), ACT.Copy)
+        nc.vector.tensor_copy(*w_views(1))
         copy_out(last)
         quantise_w(0)
         quantise_v(last - 1)
@@ -113,21 +105,14 @@ def tile_attend_wsum_soft_f_srt_kernel(tc, vT, wT, offs, out):
         for h in range(q_blocks):
             product(h, last)
 
-        negated = keep.tile([P, FEATURES], F32, name="negated", align_bytes=64)
-        early_max = keep.tile([P, 1], F32, name="early_max")
-        neg_max = [keep.tile([P, 1], F32, name="neg_max%d" % h) for h in range(q_blocks)]
-        expd = [keep.tile([P, FEATURES], F32, name="expd%d" % h, align_bytes=64) for h in range(q_blocks)]
-        probs = [keep.tile([P, FEATURES], F32, name="probs%d" % h, align_bytes=64) for h in range(q_blocks)]
-        total = [keep.tile([P, 1], F32, name="total%d" % h) for h in range(q_blocks)]
-        inv = [keep.tile([P, 1], F32, name="inv%d" % h) for h in range(q_blocks)]
-        nc.vector.tensor_scalar(negated[:, :early], logits[0][:, :early], -1.0, None, ALU.mult, ALU.min, accum_out=early_max[:])
-        nc.vector.tensor_scalar(negated[:, early:], logits_last[:], -1.0, early_max[:], ALU.mult, ALU.min, accum_out=neg_max[0][:])
-        nc.vector.tensor_reduce(neg_max[1][:], logits[1][:], AXIS.X, ALU.max, negate=True)
-        nc.scalar.activation(expd[0][:], negated[:], ACT.Exp, bias=neg_max[0][:], scale=-1.0, accum_out=total[0][:])
-        nc.scalar.activation(expd[1][:], logits[1][:], ACT.Exp, bias=neg_max[1][:], scale=1.0, accum_out=total[1][:])
-        nc.vector.reciprocal(inv[0][:], total[0][:])
-        nc.vector.tensor_scalar(probs[0][:], expd[0][:], inv[0][:], None, ALU.mult)
-        nc.sync.dma_start(out[0, :P, :], probs[0][:])
-        nc.vector.reciprocal(inv[1][:], total[1][:])
-        nc.vector.tensor_scalar(probs[1][:], expd[1][:], inv[1][:], None, ALU.mult)
-        nc.sync.dma_start(out[0, P:, :], probs[1][:])
+        for h in range(q_blocks):
+            neg_max = keep.tile([P, 1], F32, name="neg_max%d" % h)
+            nc.vector.tensor_reduce(neg_max[:], logits[h][:], AXIS.X, ALU.max, negate=True)
+            expd = keep.tile([P, FEATURES], F32, name="expd%d" % h)
+            total = keep.tile([P, 1], F32, name="total%d" % h)
+            nc.scalar.activation(expd[:], logits[h][:], ACT.Exp, bias=neg_max[:], scale=1.0, accum_out=total[:])
+            inv = keep.tile([P, 1], F32, name="inv%d" % h)
+            nc.vector.reciprocal(inv[:], total[:])
+            probs = keep.tile([P, FEATURES], F32, name="probs%d" % h)
+            nc.vector.tensor_scalar(probs[:], expd[:], inv[:], None, ALU.mult)
+            nc.sync.dma_start(out[0, h * P:(h + 1) * P, :], probs[:])

@@ -66,7 +66,7 @@ def tile_attend_wsum_soft_f_srt_kernel(tc, vT, wT, offs, out):
                                      ACT.Copy)
 
         def quantise_v(b):
-            v_codes[b] = keep.tile([P, P], U32, name="v_codes%d" % b, tag=["pool1", "pool2", "w_raw", "w_bf1"][b], align_bytes=64)
+            v_codes[b] = keep.tile([P, P], U32, name="v_codes%d" % b, tag=["pool1", "pool2", "pool3", "w_bf0"][b], align_bytes=64)
             nc.vector.quantize_mx(out=v_codes[b][:].bitcast(FP8X4), scales=v_scales[:, b * P:(b + 1) * P], in_=v_bf[b][:])
 
         def quantise_w(h):
@@ -90,20 +90,18 @@ def tile_attend_wsum_soft_f_srt_kernel(tc, vT, wT, offs, out):
             turn(b)
             if b < last:
                 copy_out(b)
-            if 0 < b < last:
+            if b > 0:
                 quantise_v(b - 1)
         nc.vector.tensor_copy(*w_views(0))
         nc.vector.tensor_copy(*w_views(1))
         copy_out(last)
         quantise_w(0)
-        quantise_v(last - 1)
         quantise_w(1)
         quantise_v(last)
-        for h in range(q_blocks):
-            for b in range(last):
-                product(h, b)
-        for h in range(q_blocks):
-            product(h, last)
+        for b in range(e_blocks):
+            product(0, b)
+        for b in reversed(range(e_blocks)):
+            product(1, b)
 
         for h in range(q_blocks):
             neg_max = keep.tile([P, 1], F32, name="neg_max%d" % h)

@@ -66,7 +66,7 @@ def tile_attend_wsum_soft_f_srt_kernel(tc, vT, wT, offs, out):
                                      ACT.Copy)
 
         def quantise_v(b):
-            v_codes[b] = keep.tile([P, P], U32, name="v_codes%d" % b, tag=["pool1", "pool2", "pool3", "w_bf0"][b], align_bytes=64)
+            v_codes[b] = keep.tile([P, P], U32, name="v_codes%d" % b, tag=["pool1", "pool2", "w_raw", "w_bf0"][b], align_bytes=64)
             nc.vector.quantize_mx(out=v_codes[b][:].bitcast(FP8X4), scales=v_scales[:, b * P:(b + 1) * P], in_=v_bf[b][:])
 
         def quantise_w(h):
@@ -90,14 +90,15 @@ def tile_attend_wsum_soft_f_srt_kernel(tc, vT, wT, offs, out):
             turn(b)
             if b < last:
                 copy_out(b)
-            if b > 0:
+            if 0 < b < last:
                 quantise_v(b - 1)
         nc.vector.tensor_copy(*w_views(0))
         nc.vector.tensor_copy(*w_views(1))
         copy_out(last)
         quantise_w(0)
-        quantise_w(1)
+        quantise_v(last - 1)
         quantise_v(last)
+        quantise_w(1)
         for b in range(e_blocks):
             product(0, b)
         for b in reversed(range(e_blocks)):
@@ -112,5 +113,8 @@ def tile_attend_wsum_soft_f_srt_kernel(tc, vT, wT, offs, out):
             inv = keep.tile([P, 1], F32, name="inv%d" % h)
             nc.vector.reciprocal(inv[:], total[:])
             probs = keep.tile([P, FEATURES], F32, name="probs%d" % h)
-            nc.vector.tensor_scalar(probs[:], expd[:], inv[:], None, ALU.mult)
+            split = FEATURES if h == 0 else last * P
+            nc.vector.tensor_scalar(probs[:, :split], expd[:, :split], inv[:], None, ALU.mult)
+            if split < FEATURES:
+                nc.scalar.activation(probs[:, split:], expd[:, split:], ACT.Copy, scale=inv[:])
             nc.sync.dma_start(out[0, h * P:(h + 1) * P, :], probs[:])

@@ -66,8 +66,9 @@ def tile_attend_wsum_soft_f_srt_kernel(tc, vT, wT, offs, out):
                                      ACT.Copy)
 
         def quantise_v(b):
-            v_codes[b] = keep.tile([P, P], U32, name="v_codes%d" % b, tag=["pool1", "pool2", "w_raw", "w_bf0"][b], align_bytes=64)
-            nc.vector.quantize_mx(out=v_codes[b][:].bitcast(FP8X4), scales=v_scales[:, b * P:(b + 1) * P], in_=v_bf[b][:])
+            if b % 2 == 0:
+                v_codes[b // 2] = keep.tile([P, 2 * P], U32, name="v_codes%d" % b, tag=["pool2", "w_raw"][b // 2], align_bytes=64)
+            nc.vector.quantize_mx(out=v_codes[b // 2][:, b % 2 * P:(b % 2 + 1) * P].bitcast(FP8X4), scales=v_scales[:, b * P:(b + 1) * P], in_=v_bf[b][:])
 
         def quantise_w(h):
             rows = slice(h * P, (h + 1) * P)
@@ -79,19 +80,20 @@ def tile_attend_wsum_soft_f_srt_kernel(tc, vT, wT, offs, out):
 
         logits = [psum.tile([P, FEATURES], F32, name="logits%d" % h) for h in range(q_blocks)]
 
-        def product(h, b):
+        def product(h, b, blocks):
             rows = slice(h * P, (h + 1) * P)
-            cols = slice(b * P, (b + 1) * P)
+            cols = slice(b * P, (b + blocks) * P)
             nc.tensor.matmul_mx(out=logits[h][:, cols], lhsT=w_codes[:, rows].bitcast(FP8X4), lhsT_scale=w_scales[:, rows],
-                                rhs=v_codes[b][:].bitcast(FP8X4), rhs_scale=v_scales[:, cols], start=True, stop=True)
+                                rhs=v_codes[b // 2][:, b % 2 * P:(b % 2 + blocks) * P].bitcast(FP8X4), rhs_scale=v_scales[:, cols], start=True, stop=True)
 
         for b in range(e_blocks):
             gather(b)
             turn(b)
             if b < last:
                 copy_out(b)
-            if 0 < b < last:
-                quantise_v(b - 1)
+            if b == last - 1:
+                quantise_v(0)
+                quantise_v(1)
         nc.vector.tensor_copy(*w_views(0))
         nc.vector.tensor_copy(*w_views(1))
         copy_out(last)
@@ -99,10 +101,11 @@ def tile_attend_wsum_soft_f_srt_kernel(tc, vT, wT, offs, out):
         quantise_v(last - 1)
         quantise_v(last)
         quantise_w(1)
-        for b in range(e_blocks):
-            product(0, b)
-        for b in reversed(range(e_blocks)):
-            product(1, b)
+        product(0, 0, 2)
+        product(0, 2, 1)
+        product(0, 3, 1)
+        product(1, 2, 2)
+        product(1, 0, 2)
 
         for h in range(q_blocks):
             neg_max = keep.tile([P, 1], F32, name="neg_max%d" % h)

@@ -78,12 +78,15 @@ def tile_attend_wsum_soft_f_srt_kernel(tc, vT, wT, offs, out):
             return (w_bf[h][:].rearrange("p (c i) j -> p c j i", i=4),
                     w_raw[:, :, h * P:(h + 1) * P].rearrange("p j (c i) -> p c j i", i=4))
 
-        logits = [psum.tile([P, FEATURES], F32, name="logits%d" % h) for h in range(q_blocks)]
+        half = FEATURES // 2
+        first = [psum.tile([P, half], F32, name="first%d" % a) for a in range(2)]
+        second = psum.tile([P, FEATURES], F32, name="second")
 
         def product(h, b, blocks):
             rows = slice(h * P, (h + 1) * P)
             cols = slice(b * P, (b + blocks) * P)
-            nc.tensor.matmul_mx(out=logits[h][:, cols], lhsT=w_codes[:, rows].bitcast(FP8X4), lhsT_scale=w_scales[:, rows],
+            target = second[:, cols] if h == 1 else first[b // 2][:, b % 2 * P:(b % 2 + blocks) * P]
+            nc.tensor.matmul_mx(out=target, lhsT=w_codes[:, rows].bitcast(FP8X4), lhsT_scale=w_scales[:, rows],
                                 rhs=v_codes[b // 2][:, b % 2 * P:(b % 2 + blocks) * P].bitcast(FP8X4), rhs_scale=v_scales[:, cols], start=True, stop=True)
 
         for b in range(e_blocks):
@@ -99,20 +102,30 @@ def tile_attend_wsum_soft_f_srt_kernel(tc, vT, wT, offs, out):
         copy_out(last)
         quantise_w(0)
         quantise_v(last - 1)
-        quantise_v(last)
         quantise_w(1)
+        quantise_v(last)
         product(0, 0, 2)
         product(0, 2, 1)
+        product(1, 0, 1)
         product(0, 3, 1)
         product(1, 2, 2)
-        product(1, 0, 2)
+        product(1, 1, 1)
 
         for h in range(q_blocks):
             neg_max = keep.tile([P, 1], F32, name="neg_max%d" % h)
-            nc.vector.tensor_reduce(neg_max[:], logits[h][:], AXIS.X, ALU.max, negate=True)
+            if h == 0:
+                negated = keep.tile([P, FEATURES], F32, name="negated")
+                neg_early = keep.tile([P, 1], F32, name="neg_early")
+                nc.vector.tensor_scalar(negated[:, :half], first[0][:], -1.0, None, ALU.mult, ALU.min, accum_out=neg_early[:])
+                nc.vector.tensor_scalar(negated[:, half:], first[1][:], -1.0, neg_early[:], ALU.mult, ALU.min, accum_out=neg_max[:])
+            else:
+                nc.vector.tensor_reduce(neg_max[:], second[:], AXIS.X, ALU.max, negate=True)
             expd = keep.tile([P, FEATURES], F32, name="expd%d" % h)
             total = keep.tile([P, 1], F32, name="total%d" % h)
-            nc.scalar.activation(expd[:], logits[h][:], ACT.Exp, bias=neg_max[:], scale=1.0, accum_out=total[:])
+            if h == 0:
+                nc.scalar.activation(expd[:], negated[:], ACT.Exp, bias=neg_max[:], scale=-1.0, accum_out=total[:])
+            else:
+                nc.scalar.activation(expd[:], second[:], ACT.Exp, bias=neg_max[:], scale=1.0, accum_out=total[:])
             inv = keep.tile([P, 1], F32, name="inv%d" % h)
             nc.vector.reciprocal(inv[:], total[:])
             probs = keep.tile([P, FEATURES], F32, name="probs%d" % h)

@@ -49,12 +49,12 @@ def tile_attend_wsum_soft_f_srt_kernel(tc, vT, wT, offs, out):
         v_bf, v_codes = {}, {}
 
         def gather(b):
-            nc.vector.tensor_copy(picked[b][:], pools[b][:].indirect(offsets[:]))
+            nc.vector.tensor_copy(picked[b][:].rearrange("p (u r i) -> p r u i", u=2, i=2), pools[b][:].indirect(offsets[:]))
 
         def turn(b):
             words = picked[b][:].bitcast(F32)
             for u in range(2):
-                nc.tensor.transpose(turned[b][:, u, :], words[:, u::2], ident[:])
+                nc.tensor.transpose(turned[b][:, u, :], words[:, u * P:(u + 1) * P], ident[:])
 
         def copy_out(b):
             v_bf[b] = keep.tile([P, 4 * P], BF16, name="v_bf%d" % b, align_bytes=64)

@@ -28,13 +28,16 @@ def tile_attend_wsum_soft_f_srt_kernel(tc, vT, wT, offs, out):
         psum = ctx.enter_context(tc.psum_pool(name="psum", bufs=1))
 
         offsets = keep.tile([P, SLOTS // 16], U16, name="offsets")
-        pools = [keep.tile([P, TOKENS], F32, name="pool%d" % b, tag="pool%d" % b, align_bytes=64) for b in range(e_blocks)]
+        pool01 = keep.tile([P, 2, TOKENS], F32, name="pool01", align_bytes=64)
+        pools = [pool01[:, 0, :], pool01[:, 1, :]] + [keep.tile([P, TOKENS], F32, name="pool%d" % b, tag="pool%d" % b, align_bytes=64)[:] for b in range(2, e_blocks)]
         w_raw = keep.tile([P, 4, QUERIES], F32, name="w_raw", tag="w_raw", align_bytes=64)
-        nc.sync.dma_start(pools[0][:], vT[0:P, :])
+        nc.sync.dma_start(pool01[:], vT[0:2 * P, :].rearrange("(b p) t -> p b t", b=2))
         nc.sync.dma_start(offsets[:], offs)
-        for b in range(1, last):
-            nc.sync.dma_start(pools[b][:], vT[b * P:(b + 1) * P, :])
-        nc.sync.dma_start(pools[last][:], vT[last * P:, :])
+        nc.sync.dma_start(pools[2], vT[2 * P:3 * P, :])
+        early_slots = 256
+        prefix = TOKENS - SLOTS + early_slots
+        nc.sync.dma_start(pools[last][:, :prefix], vT[last * P:, :prefix])
+        nc.sync.dma_start(pools[last][:, prefix:], vT[last * P:, prefix:])
         nc.sync.dma_start(w_raw[:], wT[0].rearrange("(p j) q -> p j q", j=4))
 
         ident = keep.tile([P, P], F32, name="ident")
@@ -49,7 +52,12 @@ def tile_attend_wsum_soft_f_srt_kernel(tc, vT, wT, offs, out):
         v_bf, v_codes = {}, {}
 
         def gather(b):
-            nc.vector.tensor_copy(picked[b][:].rearrange("p (u r i) -> p r u i", u=2, i=2), pools[b][:].indirect(offsets[:]))
+            dealt = picked[b][:].rearrange("p (u r i) -> p r u i", u=2, i=2)
+            if b < last:
+                nc.vector.tensor_copy(dealt, pools[b].indirect(offsets[:]))
+            else:
+                nc.vector.tensor_copy(dealt[:, :early_slots // 4], pools[b][:, :prefix].indirect(offsets[:, :early_slots // 16]))
+                nc.vector.tensor_copy(dealt[:, early_slots // 4:], pools[b].indirect(offsets[:, early_slots // 16:]))
 
         def turn(b):
             words = picked[b][:].bitcast(F32)
@@ -66,9 +74,12 @@ def tile_attend_wsum_soft_f_srt_kernel(tc, vT, wT, offs, out):
                                      ACT.Copy)
 
         def quantise_v(b):
-            if b % 2 == 0:
-                v_codes[b // 2] = keep.tile([P, 2 * P], U32, name="v_codes%d" % b, tag=["pool2", "w_raw"][b // 2], align_bytes=64)
-            nc.vector.quantize_mx(out=v_codes[b // 2][:, b % 2 * P:(b % 2 + 1) * P].bitcast(FP8X4), scales=v_scales[:, b * P:(b + 1) * P], in_=v_bf[b][:])
+            if b == 0:
+                pair = keep.tile([P, 2 * P], U32, name="v_codes01", tag="pool2", align_bytes=64)
+                v_codes[0], v_codes[1] = pair[:], pair[:, P:]
+            if b >= 2:
+                v_codes[b] = keep.tile([P, P], U32, name="v_codes%d" % b, tag={2: "pool3", 3: "w_raw"}[b], align_bytes=64)[:]
+            nc.vector.quantize_mx(out=v_codes[b][:, :P].bitcast(FP8X4), scales=v_scales[:, b * P:(b + 1) * P], in_=v_bf[b][:])
 
         def quantise_w(h):
             rows = slice(h * P, (h + 1) * P)
@@ -78,16 +89,21 @@ def tile_attend_wsum_soft_f_srt_kernel(tc, vT, wT, offs, out):
             return (w_bf[h][:].rearrange("p (c i) j -> p c j i", i=4),
                     w_raw[:, :, h * P:(h + 1) * P].rearrange("p j (c i) -> p c j i", i=4))
 
-        half = FEATURES // 2
-        first = [psum.tile([P, half], F32, name="first%d" % a) for a in range(2)]
+        half = P
+        first = [psum.tile([P, P], F32, name="first0"), psum.tile([P, last * P], F32, name="first1")]
         second = psum.tile([P, FEATURES], F32, name="second")
 
         def product(h, b, blocks):
             rows = slice(h * P, (h + 1) * P)
             cols = slice(b * P, (b + blocks) * P)
-            target = second[:, cols] if h == 1 else first[b // 2][:, b % 2 * P:(b % 2 + blocks) * P]
+            if h == 1:
+                target = second[:, cols]
+            elif b == 0:
+                target = first[0][:]
+            else:
+                target = first[1][:, (b - 1) * P:(b - 1 + blocks) * P]
             nc.tensor.matmul_mx(out=target, lhsT=w_codes[:, rows].bitcast(FP8X4), lhsT_scale=w_scales[:, rows],
-                                rhs=v_codes[b // 2][:, b % 2 * P:(b % 2 + blocks) * P].bitcast(FP8X4), rhs_scale=v_scales[:, cols], start=True, stop=True)
+                                rhs=v_codes[b][:, :blocks * P].bitcast(FP8X4), rhs_scale=v_scales[:, cols], start=True, stop=True)
 
         for b in range(e_blocks):
             gather(b)
@@ -97,19 +113,18 @@ def tile_attend_wsum_soft_f_srt_kernel(tc, vT, wT, offs, out):
             if b == last - 1:
                 quantise_v(0)
                 quantise_v(1)
+        quantise_v(last - 1)
         nc.vector.tensor_copy(*w_views(0))
         nc.vector.tensor_copy(*w_views(1))
         copy_out(last)
         quantise_w(0)
-        quantise_v(last - 1)
         quantise_w(1)
         quantise_v(last)
-        product(0, 0, 2)
-        product(0, 2, 1)
-        product(1, 0, 1)
-        product(0, 3, 1)
-        product(1, 2, 2)
-        product(1, 1, 1)
+        for b in range(e_blocks):
+            product(0, b, 1)
+        product(1, 3, 1)
+        product(1, 2, 1)
+        product(1, 0, 2)
 
         for h in range(q_blocks):
             neg_max = keep.tile([P, 1], F32, name="neg_max%d" % h)

@@ -30,7 +30,10 @@ def tile_attend_wsum_soft_f_srt_kernel(tc, vT, wT, offs, out):
         offsets = keep.tile([P, SLOTS // 16], U16, name="offsets")
         pool01 = keep.tile([P, 2, TOKENS], F32, name="pool01", align_bytes=64)
         pools = [pool01[:, 0, :], pool01[:, 1, :]] + [keep.tile([P, TOKENS], F32, name="pool%d" % b, tag="pool%d" % b, align_bytes=64)[:] for b in range(2, e_blocks)]
-        w_raw = keep.tile([P, 4, QUERIES], F32, name="w_raw", tag="w_raw", align_bytes=64)
+        part = P // 2
+        ahead = 2 * P - part
+        w_tile = keep.tile([P, ahead + 4 * QUERIES], F32, name="w_tile", align_bytes=64)
+        w_raw = w_tile[:, ahead:].rearrange("p (j q) -> p j q", j=4)
         nc.sync.dma_start(pool01[:], vT[0:2 * P, :].rearrange("(b p) t -> p b t", b=2))
         nc.sync.dma_start(offsets[:], offs)
         nc.sync.dma_start(pools[2], vT[2 * P:3 * P, :])
@@ -38,7 +41,7 @@ def tile_attend_wsum_soft_f_srt_kernel(tc, vT, wT, offs, out):
         prefix = TOKENS - SLOTS + early_slots
         nc.sync.dma_start(pools[last][:, :prefix], vT[last * P:, :prefix])
         nc.sync.dma_start(pools[last][:, prefix:], vT[last * P:, prefix:])
-        nc.sync.dma_start(w_raw[:], wT[0].rearrange("(p j) q -> p j q", j=4))
+        nc.sync.dma_start(w_raw, wT[0].rearrange("(p j) q -> p j q", j=4))
 
         ident = keep.tile([P, P], F32, name="ident")
         make_identity(nc, ident[:])
@@ -48,7 +51,7 @@ def tile_attend_wsum_soft_f_srt_kernel(tc, vT, wT, offs, out):
         v_scales = keep.tile([P, FEATURES], U8, name="v_scales", align_bytes=64)
         w_scales = keep.tile([P, QUERIES], U8, name="w_scales", align_bytes=64)
         w_codes = keep.tile([P, QUERIES], U32, name="w_codes", align_bytes=64)
-        w_bf = [keep.tile([P, P, 4], BF16, name="w_bf%d" % h, tag="w_bf%d" % h, align_bytes=64) for h in range(q_blocks)]
+        w_bf = [keep.tile([P, 4 * n], BF16, name="w_bf%d" % i, align_bytes=64) for i, n in enumerate((part, part, P))]
         v_bf, v_codes = {}, {}
 
         def gather(b):
@@ -65,6 +68,10 @@ def tile_attend_wsum_soft_f_srt_kernel(tc, vT, wT, offs, out):
                 nc.tensor.transpose(turned[b][:, u, :], words[:, u * P:(u + 1) * P], ident[:])
 
         def copy_out(b):
+            if b == last:
+                v_bf[b] = w_tile[:, :2 * P].bitcast(BF16)
+                nc.scalar.copy(w_tile[:, :2 * P].rearrange("p (e u) -> p e u", u=2), turned[b][:].rearrange("p u e -> p e u"))
+                return
             v_bf[b] = keep.tile([P, 4 * P], BF16, name="v_bf%d" % b, align_bytes=64)
             if b > 0:
                 nc.scalar.copy(v_bf[b][:].bitcast(F32).rearrange("p (e u) -> p e u", u=2), turned[b][:].rearrange("p u e -> p e u"))
@@ -78,16 +85,17 @@ def tile_attend_wsum_soft_f_srt_kernel(tc, vT, wT, offs, out):
                 pair = keep.tile([P, 2 * P], U32, name="v_codes01", tag="pool2", align_bytes=64)
                 v_codes[0], v_codes[1] = pair[:], pair[:, P:]
             if b >= 2:
-                v_codes[b] = keep.tile([P, P], U32, name="v_codes%d" % b, tag={2: "pool3", 3: "w_raw"}[b], align_bytes=64)[:]
-            nc.vector.quantize_mx(out=v_codes[b][:, :P].bitcast(FP8X4), scales=v_scales[:, b * P:(b + 1) * P], in_=v_bf[b][:])
+                v_codes[b] = keep.tile([P, P], U32, name="v_codes%d" % b, tag={2: "pool3", 3: "v_codes3"}[b], align_bytes=64)[:]
+            nc.vector.quantize_mx(out=v_codes[b][:, :P].bitcast(FP8X4), scales=v_scales[:, b * P:(b + 1) * P], in_=v_bf[b][:, :])
 
-        def quantise_w(h):
-            rows = slice(h * P, (h + 1) * P)
-            nc.vector.quantize_mx(out=w_codes[:, rows].bitcast(FP8X4), scales=w_scales[:, rows], in_=w_bf[h][:].rearrange("p q j -> p (q j)"))
+        def quantise_w(i):
+            rows = slice(i * part, i * part + w_bf[i].shape[1] // 4)
+            nc.vector.quantize_mx(out=w_codes[:, rows].bitcast(FP8X4), scales=w_scales[:, rows], in_=w_bf[i][:])
 
-        def w_views(h):
-            return (w_bf[h][:].rearrange("p (c i) j -> p c j i", i=4),
-                    w_raw[:, :, h * P:(h + 1) * P].rearrange("p j (c i) -> p c j i", i=4))
+        def w_views(i):
+            target = w_bf[i][:, :4 * part] if i < 3 else w_bf[2][:, 4 * part:]
+            return (target.rearrange("p (c i j) -> p c j i", i=4, j=4),
+                    w_raw[:, :, i * part:(i + 1) * part].rearrange("p j (c i) -> p c j i", i=4))
 
         half = P
         first = [psum.tile([P, P], F32, name="first0"), psum.tile([P, last * P], F32, name="first1")]
@@ -114,11 +122,12 @@ def tile_attend_wsum_soft_f_srt_kernel(tc, vT, wT, offs, out):
                 quantise_v(0)
                 quantise_v(1)
         quantise_v(last - 1)
-        nc.vector.tensor_copy(*w_views(0))
-        nc.vector.tensor_copy(*w_views(1))
+        for i in range(3):
+            nc.vector.tensor_copy(*w_views(i))
+        nc.scalar.copy(*w_views(3))
         copy_out(last)
-        quantise_w(0)
-        quantise_w(1)
+        for i in range(3):
+            quantise_w(i)
         quantise_v(last)
         for b in range(e_blocks):
             product(0, b, 1)

@@ -34,13 +34,14 @@ def tile_attend_wsum_soft_f_srt_kernel(tc, vT, wT, offs, out):
         ahead = 2 * P - part
         w_tile = keep.tile([P, ahead + 4 * QUERIES], F32, name="w_tile", align_bytes=64)
         w_raw = w_tile[:, ahead:].rearrange("p (j q) -> p j q", j=4)
-        nc.sync.dma_start(pool01[:], vT[0:2 * P, :].rearrange("(b p) t -> p b t", b=2))
+        nc.sync.dma_start(pool01[:], vT[0:2 * P, :].rearrange("(p b) t -> p b t", b=2))
         nc.sync.dma_start(offsets[:], offs)
-        nc.sync.dma_start(pools[2], vT[2 * P:3 * P, :])
+        upper = vT[2 * P:, :].rearrange("(p b) t -> b p t", b=2)
+        nc.sync.dma_start(pools[2], upper[0])
         early_slots = 256
         prefix = TOKENS - SLOTS + early_slots
-        nc.sync.dma_start(pools[last][:, :prefix], vT[last * P:, :prefix])
-        nc.sync.dma_start(pools[last][:, prefix:], vT[last * P:, prefix:])
+        nc.sync.dma_start(pools[last][:, :prefix], upper[1][:, :prefix])
+        nc.sync.dma_start(pools[last][:, prefix:], upper[1][:, prefix:])
         nc.sync.dma_start(w_raw, wT[0].rearrange("(p j) q -> p j q", j=4))
 
         ident = keep.tile([P, P], F32, name="ident")
@@ -147,9 +148,9 @@ def tile_attend_wsum_soft_f_srt_kernel(tc, vT, wT, offs, out):
             expd = keep.tile([P, FEATURES], F32, name="expd%d" % h)
             total = keep.tile([P, 1], F32, name="total%d" % h)
             if h == 0:
-                nc.scalar.activation(expd[:], negated[:], ACT.Exp, bias=neg_max[:], scale=-1.0, accum_out=total[:])
+                nc.scalar.activation(expd[:].rearrange("p (g e b) -> p g e b", g=2, b=2), negated[:].rearrange("p (g b e) -> p g e b", g=2, b=2), ACT.Exp, bias=neg_max[:], scale=-1.0, accum_out=total[:])
             else:
-                nc.scalar.activation(expd[:], second[:], ACT.Exp, bias=neg_max[:], scale=1.0, accum_out=total[:])
+                nc.scalar.activation(expd[:].rearrange("p (g e b) -> p g e b", g=2, b=2), second[:].rearrange("p (g b e) -> p g e b", g=2, b=2), ACT.Exp, bias=neg_max[:], scale=1.0, accum_out=total[:])
             inv = keep.tile([P, 1], F32, name="inv%d" % h)
             nc.vector.reciprocal(inv[:], total[:])
             probs = keep.tile([P, FEATURES], F32, name="probs%d" % h)

@@ -30,8 +30,8 @@ def tile_attend_wsum_soft_f_srt_kernel(tc, vT, wT, offs, out):
         offsets = keep.tile([P, SLOTS // 16], U16, name="offsets")
         pool01 = keep.tile([P, 2, TOKENS], F32, name="pool01", align_bytes=64)
         pools = [pool01[:, 0, :], pool01[:, 1, :]] + [keep.tile([P, TOKENS], F32, name="pool%d" % b, tag="pool%d" % b, align_bytes=64)[:] for b in range(2, e_blocks)]
-        part = P // 2
-        ahead = 2 * P - part
+        lead, shared, part = 32, 80, P // 2
+        ahead = 2 * P - lead
         w_tile = keep.tile([P, ahead + 4 * QUERIES], F32, name="w_tile", align_bytes=64)
         w_raw = w_tile[:, ahead:].rearrange("p (j q) -> p j q", j=4)
         nc.sync.dma_start(pool01[:], vT[0:2 * P, :].rearrange("(p b) t -> p b t", b=2))
@@ -52,7 +52,9 @@ def tile_attend_wsum_soft_f_srt_kernel(tc, vT, wT, offs, out):
         v_scales = keep.tile([P, FEATURES], U8, name="v_scales", align_bytes=64)
         w_scales = keep.tile([P, QUERIES], U8, name="w_scales", align_bytes=64)
         w_codes = keep.tile([P, QUERIES], U32, name="w_codes", align_bytes=64)
-        w_bf = [keep.tile([P, 4 * n], BF16, name="w_bf%d" % i, align_bytes=64) for i, n in enumerate((part, part, P))]
+        w_bf = {0: keep.tile([P, 4 * P], BF16, name="w_bf0", align_bytes=64)[:],
+                P: keep.tile([P, 4 * part], BF16, name="w_bf1", align_bytes=64)[:],
+                P + part: w_raw[:, 1, :P].bitcast(BF16)}
         v_bf, v_codes = {}, {}
 
         def gather(b):
@@ -89,14 +91,13 @@ def tile_attend_wsum_soft_f_srt_kernel(tc, vT, wT, offs, out):
                 v_codes[b] = keep.tile([P, P], U32, name="v_codes%d" % b, tag={2: "pool3", 3: "v_codes3"}[b], align_bytes=64)[:]
             nc.vector.quantize_mx(out=v_codes[b][:, :P].bitcast(FP8X4), scales=v_scales[:, b * P:(b + 1) * P], in_=v_bf[b][:, :])
 
-        def quantise_w(i):
-            rows = slice(i * part, i * part + w_bf[i].shape[1] // 4)
-            nc.vector.quantize_mx(out=w_codes[:, rows].bitcast(FP8X4), scales=w_scales[:, rows], in_=w_bf[i][:])
+        def quantise_w(start):
+            rows = slice(start, start + w_bf[start].shape[1] // 4)
+            nc.vector.quantize_mx(out=w_codes[:, rows].bitcast(FP8X4), scales=w_scales[:, rows], in_=w_bf[start])
 
-        def w_views(i):
-            target = w_bf[i][:, :4 * part] if i < 3 else w_bf[2][:, 4 * part:]
-            return (target.rearrange("p (c i j) -> p c j i", i=4, j=4),
-                    w_raw[:, :, i * part:(i + 1) * part].rearrange("p j (c i) -> p c j i", i=4))
+        def w_views(base, start, stop):
+            return (w_bf[base][:, 4 * (start - base):4 * (stop - base)].rearrange("p (c i j) -> p c j i", i=4, j=4),
+                    w_raw[:, :, start:stop].rearrange("p j (c i) -> p c j i", i=4))
 
         half = P
         first = [psum.tile([P, P], F32, name="first0"), psum.tile([P, last * P], F32, name="first1")]
@@ -123,13 +124,16 @@ def tile_attend_wsum_soft_f_srt_kernel(tc, vT, wT, offs, out):
                 quantise_v(0)
                 quantise_v(1)
         quantise_v(last - 1)
-        for i in range(3):
-            nc.vector.tensor_copy(*w_views(i))
-        nc.scalar.copy(*w_views(3))
+        nc.vector.tensor_copy(*w_views(0, 0, lead))
+        nc.vector.tensor_copy(*w_views(0, lead, shared))
+        nc.scalar.copy(*w_views(0, shared, P))
+        nc.vector.tensor_copy(*w_views(P, P, P + part))
         copy_out(last)
-        for i in range(3):
-            quantise_w(i)
+        quantise_w(0)
+        nc.vector.tensor_copy(*w_views(P + part, P + part, QUERIES))
         quantise_v(last)
+        quantise_w(P)
+        quantise_w(P + part)
         for b in range(e_blocks):
             product(0, b, 1)
         product(1, 3, 1)
@@ -139,7 +143,7 @@ def tile_attend_wsum_soft_f_srt_kernel(tc, vT, wT, offs, out):
         for h in range(q_blocks):
             neg_max = keep.tile([P, 1], F32, name="neg_max%d" % h)
             if h == 0:
-                negated = keep.tile([P, FEATURES], F32, name="negated")
+                negated = w_tile[:, ahead + QUERIES + P:ahead + QUERIES + P + FEATURES]
                 neg_early = keep.tile([P, 1], F32, name="neg_early")
                 nc.vector.tensor_scalar(negated[:, :half], first[0][:], -1.0, None, ALU.mult, ALU.min, accum_out=neg_early[:])
                 nc.vector.tensor_scalar(negated[:, half:], first[1][:], -1.0, neg_early[:], ALU.mult, ALU.min, accum_out=neg_max[:])
@@ -148,7 +152,7 @@ def tile_attend_wsum_soft_f_srt_kernel(tc, vT, wT, offs, out):
             expd = keep.tile([P, FEATURES], F32, name="expd%d" % h)
             total = keep.tile([P, 1], F32, name="total%d" % h)
             if h == 0:
-                nc.scalar.activation(expd[:].rearrange("p (g e b) -> p g e b", g=2, b=2), negated[:].rearrange("p (g b e) -> p g e b", g=2, b=2), ACT.Exp, bias=neg_max[:], scale=-1.0, accum_out=total[:])
+                nc.scalar.activation(expd[:].rearrange("p (g e b) -> p g e b", g=2, b=2), negated.rearrange("p (g b e) -> p g e b", g=2, b=2), ACT.Exp, bias=neg_max[:], scale=-1.0, accum_out=total[:])
             else:
                 nc.scalar.activation(expd[:].rearrange("p (g e b) -> p g e b", g=2, b=2), second[:].rearrange("p (g b e) -> p g e b", g=2, b=2), ACT.Exp, bias=neg_max[:], scale=1.0, accum_out=total[:])
             inv = keep.tile([P, 1], F32, name="inv%d" % h)

@@ -15,6 +15,7 @@ AXIS = mybir.AxisListType
 
 P = 128
 SLOTS, TOKENS, QUERIES, FEATURES = 512, 2048, 256, 512
+DMA_ALIGN = 512
 FLOPS = 2 * QUERIES * SLOTS * FEATURES
 
 
@@ -27,12 +28,12 @@ def tile_attend_wsum_soft_f_srt_kernel(tc, vT, wT, offs, out):
         keep = ctx.enter_context(tc.tile_pool(name="keep", bufs=1))
         psum = ctx.enter_context(tc.psum_pool(name="psum", bufs=1))
 
-        offsets = keep.tile([P, SLOTS // 16], U16, name="offsets")
-        pool01 = keep.tile([P, 2, TOKENS], F32, name="pool01", align_bytes=64)
-        pools = [pool01[:, 0, :], pool01[:, 1, :]] + [keep.tile([P, TOKENS], F32, name="pool%d" % b, tag="pool%d" % b, align_bytes=64)[:] for b in range(2, e_blocks)]
+        offsets = keep.tile([P, SLOTS // 16], U16, name="offsets", align_bytes=DMA_ALIGN)
+        pool01 = keep.tile([P, 2, TOKENS], F32, name="pool01", align_bytes=DMA_ALIGN)
+        pools = [pool01[:, 0, :], pool01[:, 1, :]] + [keep.tile([P, TOKENS], F32, name="pool%d" % b, tag="pool%d" % b, align_bytes=DMA_ALIGN)[:] for b in range(2, e_blocks)]
         lead, shared, part = 32, 80, P // 2
-        ahead = 2 * P - lead
-        w_tile = keep.tile([P, ahead + 4 * QUERIES], F32, name="w_tile", align_bytes=64)
+        ahead = 2 * P
+        w_tile = keep.tile([P, ahead + 4 * QUERIES], F32, name="w_tile", align_bytes=DMA_ALIGN)
         w_raw = w_tile[:, ahead:].rearrange("p (j q) -> p j q", j=4)
         nc.sync.dma_start(pool01[:], vT[0:2 * P, :].rearrange("(p b) t -> p b t", b=2))
         nc.sync.dma_start(offsets[:], offs)
@@ -72,8 +73,8 @@ def tile_attend_wsum_soft_f_srt_kernel(tc, vT, wT, offs, out):
 
         def copy_out(b):
             if b == last:
-                v_bf[b] = w_tile[:, :2 * P].bitcast(BF16)
-                nc.scalar.copy(w_tile[:, :2 * P].rearrange("p (e u) -> p e u", u=2), turned[b][:].rearrange("p u e -> p e u"))
+                v_bf[b] = w_tile[:, lead:lead + 2 * P].bitcast(BF16)
+                nc.scalar.copy(w_tile[:, lead:lead + 2 * P].rearrange("p (e u) -> p e u", u=2), turned[b][:].rearrange("p u e -> p e u"))
                 return
             v_bf[b] = keep.tile([P, 4 * P], BF16, name="v_bf%d" % b, align_bytes=64)
             if b > 0:
@@ -85,10 +86,11 @@ def tile_attend_wsum_soft_f_srt_kernel(tc, vT, wT, offs, out):
 
         def quantise_v(b):
             if b == 0:
-                pair = keep.tile([P, 2 * P], U32, name="v_codes01", tag="pool2", align_bytes=64)
+                pair = keep.tile([P, 2 * P], U32, name="v_codes01", tag="pool2", align_bytes=DMA_ALIGN)
                 v_codes[0], v_codes[1] = pair[:], pair[:, P:]
-            if b >= 2:
-                v_codes[b] = keep.tile([P, P], U32, name="v_codes%d" % b, tag={2: "pool3", 3: "v_codes3"}[b], align_bytes=64)[:]
+            if b == 2:
+                pair = keep.tile([P, 2 * P], U32, name="v_codes23", tag="pool3", align_bytes=DMA_ALIGN)
+                v_codes[2], v_codes[3] = pair[:], pair[:, P:]
             nc.vector.quantize_mx(out=v_codes[b][:, :P].bitcast(FP8X4), scales=v_scales[:, b * P:(b + 1) * P], in_=v_bf[b][:, :])
 
         def quantise_w(start):
@@ -136,8 +138,7 @@ def tile_attend_wsum_soft_f_srt_kernel(tc, vT, wT, offs, out):
         quantise_w(P + part)
         for b in range(e_blocks):
             product(0, b, 1)
-        product(1, 3, 1)
-        product(1, 2, 1)
+        product(1, 2, 2)
         product(1, 0, 2)
 
         for h in range(q_blocks):
@@ -157,7 +158,7 @@ def tile_attend_wsum_soft_f_srt_kernel(tc, vT, wT, offs, out):
                 nc.scalar.activation(expd[:].rearrange("p (g e b) -> p g e b", g=2, b=2), second[:].rearrange("p (g b e) -> p g e b", g=2, b=2), ACT.Exp, bias=neg_max[:], scale=1.0, accum_out=total[:])
             inv = keep.tile([P, 1], F32, name="inv%d" % h)
             nc.vector.reciprocal(inv[:], total[:])
-            probs = keep.tile([P, FEATURES], F32, name="probs%d" % h)
+            probs = keep.tile([P, FEATURES], F32, name="probs%d" % h, align_bytes=DMA_ALIGN)
             split = FEATURES if h == 0 else last * P
             nc.vector.tensor_scalar(probs[:, :split], expd[:, :split], inv[:], None, ALU.mult)
             if split < FEATURES:

from contextlib import ExitStack

import concourse.mybir as mybir
from concourse.masks import make_identity

F32 = mybir.dt.float32
BF16 = mybir.dt.bfloat16
U32 = mybir.dt.uint32
U16 = mybir.dt.uint16
U8 = mybir.dt.uint8
FP8X4 = mybir.dt.float8_e4m3fn_x4
ACT = mybir.ActivationFunctionType
ALU = mybir.AluOpType
AXIS = mybir.AxisListType

P = 128
SLOTS, TOKENS, QUERIES, FEATURES = 512, 2048, 256, 512
DMA_ALIGN = 512
FLOPS = 2 * QUERIES * SLOTS * FEATURES


def tile_attend_wsum_soft_f_srt_kernel(tc, vT, wT, offs, out):
    nc = tc.nc
    e_blocks = FEATURES // P
    q_blocks = QUERIES // P
    last = e_blocks - 1
    with ExitStack() as ctx:
        keep = ctx.enter_context(tc.tile_pool(name="keep", bufs=1))
        psum = ctx.enter_context(tc.psum_pool(name="psum", bufs=1))

        offsets = keep.tile([P, SLOTS // 16], U16, name="offsets", align_bytes=DMA_ALIGN)
        pool01 = keep.tile([P, 2, TOKENS], F32, name="pool01", align_bytes=DMA_ALIGN)
        pools = [pool01[:, 0, :], pool01[:, 1, :]] + [keep.tile([P, TOKENS], F32, name="pool%d" % b, tag="pool%d" % b, align_bytes=DMA_ALIGN)[:] for b in range(2, e_blocks)]
        lead, shared, part = 32, 80, P // 2
        ahead = 2 * P
        w_tile = keep.tile([P, ahead + 4 * QUERIES], F32, name="w_tile", align_bytes=DMA_ALIGN)
        w_raw = w_tile[:, ahead:].rearrange("p (j q) -> p j q", j=4)
        nc.sync.dma_start(pool01[:], vT[0:2 * P, :].rearrange("(p b) t -> p b t", b=2))
        nc.sync.dma_start(offsets[:], offs)
        upper = vT[2 * P:, :].rearrange("(p b) t -> b p t", b=2)
        nc.sync.dma_start(pools[2], upper[0])
        early_slots = 256
        prefix = TOKENS - SLOTS + early_slots
        nc.sync.dma_start(pools[last][:, :prefix], upper[1][:, :prefix])
        nc.sync.dma_start(pools[last][:, prefix:], upper[1][:, prefix:])
        nc.sync.dma_start(w_raw, wT[0].rearrange("(p j) q -> p j q", j=4))

        ident = keep.tile([P, P], F32, name="ident")
        make_identity(nc, ident[:])

        picked = [keep.tile([P, SLOTS], BF16, name="picked%d" % b, align_bytes=64) for b in range(e_blocks)]
        turned = [psum.tile([P, 2, P], F32, name="turned%d" % b) for b in range(e_blocks)]
        v_scales = keep.tile([P, FEATURES], U8, name="v_scales", align_bytes=64)
        w_scales = keep.tile([P, QUERIES], U8, name="w_scales", align_bytes=64)
        w_codes = keep.tile([P, QUERIES], U32, name="w_codes", align_bytes=64)
        w_bf = {0: keep.tile([P, 4 * P], BF16, name="w_bf0", align_bytes=64)[:],
                P: keep.tile([P, 4 * part], BF16, name="w_bf1", align_bytes=64)[:],
                P + part: w_raw[:, 1, :P].bitcast(BF16)}
        v_bf, v_codes = {}, {}

        def gather(b):
            dealt = picked[b][:].rearrange("p (u r i) -> p r u i", u=2, i=2)
            if b < last:
                nc.vector.tensor_copy(dealt, pools[b].indirect(offsets[:]))
            else:
                nc.vector.tensor_copy(dealt[:, :early_slots // 4], pools[b][:, :prefix].indirect(offsets[:, :early_slots // 16]))
                nc.vector.tensor_copy(dealt[:, early_slots // 4:], pools[b].indirect(offsets[:, early_slots // 16:]))

        def turn(b):
            words = picked[b][:].bitcast(F32)
            for u in range(2):
                nc.tensor.transpose(turned[b][:, u, :], words[:, u * P:(u + 1) * P], ident[:])

        def copy_out(b):
            if b == last:
                v_bf[b] = w_tile[:, lead:lead + 2 * P].bitcast(BF16)
                nc.scalar.copy(w_tile[:, lead:lead + 2 * P].rearrange("p (e u) -> p e u", u=2), turned[b][:].rearrange("p u e -> p e u"))
                return
            v_bf[b] = keep.tile([P, 4 * P], BF16, name="v_bf%d" % b, align_bytes=64)
            if b > 0:
                nc.scalar.copy(v_bf[b][:].bitcast(F32).rearrange("p (e u) -> p e u", u=2), turned[b][:].rearrange("p u e -> p e u"))
            else:
                nc.scalar.activation(v_bf[b][:].rearrange("p (e u i) -> p e u i", u=2, i=2),
                                     turned[b][:].rearrange("p u e -> p (u e)").bitcast(BF16).rearrange("p (u e i) -> p e u i", u=2, i=2),
                                     ACT.Copy)

        def quantise_v(b):
            if b == 0:
                pair = keep.tile([P, 2 * P], U32, name="v_codes01", tag="pool2", align_bytes=DMA_ALIGN)
                v_codes[0], v_codes[1] = pair[:], pair[:, P:]
            if b == 2:
                pair = keep.tile([P, 2 * P], U32, name="v_codes23", tag="pool3", align_bytes=DMA_ALIGN)
                v_codes[2], v_codes[3] = pair[:], pair[:, P:]
            nc.vector.quantize_mx(out=v_codes[b][:, :P].bitcast(FP8X4), scales=v_scales[:, b * P:(b + 1) * P], in_=v_bf[b][:, :])

        def quantise_w(start):
            rows = slice(start, start + w_bf[start].shape[1] // 4)
            nc.vector.quantize_mx(out=w_codes[:, rows].bitcast(FP8X4), scales=w_scales[:, rows], in_=w_bf[start])

        def w_views(base, start, stop):
            return (w_bf[base][:, 4 * (start - base):4 * (stop - base)].rearrange("p (c i j) -> p c j i", i=4, j=4),
                    w_raw[:, :, start:stop].rearrange("p j (c i) -> p c j i", i=4))

        half = P
        first = [psum.tile([P, P], F32, name="first0"), psum.tile([P, last * P], F32, name="first1")]
        second = psum.tile([P, FEATURES], F32, name="second")

        def product(h, b, blocks):
            rows = slice(h * P, (h + 1) * P)
            cols = slice(b * P, (b + blocks) * P)
            if h == 1:
                target = second[:, cols]
            elif b == 0:
                target = first[0][:]
            else:
                target = first[1][:, (b - 1) * P:(b - 1 + blocks) * P]
            nc.tensor.matmul_mx(out=target, lhsT=w_codes[:, rows].bitcast(FP8X4), lhsT_scale=w_scales[:, rows],
                                rhs=v_codes[b][:, :blocks * P].bitcast(FP8X4), rhs_scale=v_scales[:, cols], start=True, stop=True)

        for b in range(e_blocks):
            gather(b)
            turn(b)
            if b < last:
                copy_out(b)
            if b == last - 1:
                quantise_v(0)
                quantise_v(1)
        quantise_v(last - 1)
        nc.vector.tensor_copy(*w_views(0, 0, lead))
        nc.vector.tensor_copy(*w_views(0, lead, shared))
        nc.scalar.copy(*w_views(0, shared, P))
        nc.vector.tensor_copy(*w_views(P, P, P + part))
        copy_out(last)
        quantise_w(0)
        nc.vector.tensor_copy(*w_views(P + part, P + part, QUERIES))
        quantise_v(last)
        quantise_w(P)
        quantise_w(P + part)
        for b in range(e_blocks):
            product(0, b, 1)
        product(1, 2, 2)
        product(1, 0, 2)

        for h in range(q_blocks):
            neg_max = keep.tile([P, 1], F32, name="neg_max%d" % h)
            if h == 0:
                negated = w_tile[:, ahead + QUERIES + P:ahead + QUERIES + P + FEATURES]
                neg_early = keep.tile([P, 1], F32, name="neg_early")
                nc.vector.tensor_scalar(negated[:, :half], first[0][:], -1.0, None, ALU.mult, ALU.min, accum_out=neg_early[:])
                nc.vector.tensor_scalar(negated[:, half:], first[1][:], -1.0, neg_early[:], ALU.mult, ALU.min, accum_out=neg_max[:])
            else:
                nc.vector.tensor_reduce(neg_max[:], second[:], AXIS.X, ALU.max, negate=True)
            expd = keep.tile([P, FEATURES], F32, name="expd%d" % h)
            total = keep.tile([P, 1], F32, name="total%d" % h)
            if h == 0:
                nc.scalar.activation(expd[:].rearrange("p (g e b) -> p g e b", g=2, b=2), negated.rearrange("p (g b e) -> p g e b", g=2, b=2), ACT.Exp, bias=neg_max[:], scale=-1.0, accum_out=total[:])
            else:
                nc.scalar.activation(expd[:].rearrange("p (g e b) -> p g e b", g=2, b=2), second[:].rearrange("p (g b e) -> p g e b", g=2, b=2), ACT.Exp, bias=neg_max[:], scale=1.0, accum_out=total[:])
            inv = keep.tile([P, 1], F32, name="inv%d" % h)
            nc.vector.reciprocal(inv[:], total[:])
            probs = keep.tile([P, FEATURES], F32, name="probs%d" % h, align_bytes=DMA_ALIGN)
            split = FEATURES if h == 0 else last * P
            nc.vector.tensor_scalar(probs[:, :split], expd[:, :split], inv[:], None, ALU.mult)
            if split < FEATURES:
                nc.scalar.activation(probs[:, split:], expd[:, split:], ACT.Copy, scale=inv[:])
            nc.sync.dma_start(out[0, h * P:(h + 1) * P, :], probs[:])
